import numpy as np
import ml_dtypes


def mxq(x, axis, fmt="e4m3"):
    dtype, down = {"e4m3": (ml_dtypes.float8_e4m3fn, 7), "e5m2": (ml_dtypes.float8_e5m2, 14)}[fmt]
    v = np.moveaxis(np.asarray(x, np.float32).astype(ml_dtypes.bfloat16).astype(np.float64), axis, -1)
    blocks = v.reshape(v.shape[:-1] + (-1, 32))
    amax = np.abs(blocks).max(-1, keepdims=True)
    byte = np.maximum(np.where(amax > 0, np.frexp(amax)[1] - 1 + 127, 0) - down, 1)
    scale = np.exp2(byte - 127.0)
    codes = (blocks / scale).astype(np.float32).astype(dtype).astype(np.float64)
    return np.moveaxis((codes * scale).reshape(v.shape), -1, axis)


WIDE = False


def mx_kscale(k, group=512):
    if not WIDE:
        return np.ones(k)
    levels = np.array([10, -10, 5, -5, 0])
    if group != 512:
        return np.exp2(np.random.permutation(np.resize(levels, k // group))).repeat(group)
    if k % 512:
        return np.exp2(np.random.permutation(np.resize(levels, k // 32))).repeat(32)
    a = np.empty((k // 512, 16))
    for p in range(k // 512):
        a[p, :8] = np.random.permutation(np.resize(levels, 8))
        for g in range(8):
            far = levels[np.abs(levels - a[p, g]) >= 10]
            a[p, g + 8] = far[np.random.randint(len(far))]
    return np.exp2(a.ravel()).repeat(32)


def f64(x):
    return np.asarray(x).astype(np.float64)


def gelu(v):
    return 0.5 * v * (1.0 + np.tanh(0.7978845608028654 * (v + 0.044715 * v ** 3)))


G, D, K, M, N = 4, 256, 512, 128, 512


def setup_inputs():
    n = np.random.standard_normal
    s = mx_kscale(D, 0)[:, None]
    u = mx_kscale(K)[:, None]
    return {
        "x": (n((G, D, N)) * s).astype(np.float32),
        "w1": (n((G, D, K)) / np.sqrt(D) / s).astype(np.float32),
        "hs": (np.random.uniform(0.5, 2.0, (G, K, 1)) * u).astype(np.float32),
        "w2": (n((G, K, M)) / np.sqrt(K) / u).astype(np.float32),
        "r": n((G, M, N)).astype(np.float32),
    }


def reference(x, w1, hs, w2, r):
    xq = mxq(f64(x), 1, "e4m3")
    h = mxq(f64(w1), 1, "e4m3").transpose(0, 2, 1) @ xq
    h = (gelu(h)) * f64(hs)
    y = mxq(f64(w2), 1, "e4m3").transpose(0, 2, 1) @ mxq(h, 1, "e4m3")
    y = y + f64(r)
    return y

@@ -1,0 +1,198 @@
+from contextlib import ExitStack
+
+import concourse.mybir as mybir
+
+G, D, K, M, N = 4, 256, 512, 128, 512
+FLOPS = 2 * G * N * (D * K + K * M)
+
+F32 = mybir.dt.float32
+BF16 = mybir.dt.bfloat16
+U32 = mybir.dt.uint32
+U8 = mybir.dt.uint8
+FP8X4 = mybir.dt.float8_e4m3fn_x4
+ALU = mybir.AluOpType
+ACT = mybir.ActivationFunctionType
+
+P = 128
+PACK = 4
+ROWS = D // PACK
+SIDE = P // ROWS
+PAIRS = G // SIDE
+CH = 128
+CHUNKS = N // CH
+STEPS = PAIRS * CHUNKS
+
+
+def tile_rows_gmlp_gelu_res_kernel(tc, x, w1, hs, w2, r, out):
+    nc = tc.nc
+    with ExitStack() as ctx:
+        sb = ctx.enter_context(tc.tile_pool(name="sb", bufs=1))
+        ps = ctx.enter_context(tc.psum_pool(name="ps", bufs=1))
+        ctx.enter_context(tc.manual_schedule())
+
+        def sbuf(name, shape, dtype):
+            return sb.tile(shape, dtype, name=name, align_bytes=64)
+
+        def copy_on(engine, dst, src):
+            if engine == "v":
+                nc.vector.tensor_copy(out=dst, in_=src)
+            else:
+                nc.scalar.copy(out=dst, in_=src)
+
+        def quantize(name, src, words):
+            codes = sbuf(name + "_codes", [P, words], U32)
+            scales = sbuf(name + "_scales", [P, words], U8)
+            nc.vector.quantize_mx(out=codes[:].bitcast(FP8X4), scales=scales[:], in_=src)
+            return codes, scales
+
+        z_banks = [[ps.tile([P, PACK * CH], F32, name="z%d_%d" % (c, b)) for b in range(2)] for c in range(SIDE)]
+        y_banks = [ps.tile([P, PACK * CH], F32, name="y%d" % b) for b in range(4)]
+
+        w1_raw, w1_bf, w1_q = {}, {}, {}
+        x_raw, x_bf, x_q = {}, {}, {}
+        w2_raw, w2_bf, w2_q = {}, {}, {}
+        r_sb, res = {}, {}
+        act, h_bf, h_q = {}, {}, {}
+        hs_sb = sbuf("hs_sb", [P, G, 8], F32)
+
+        def groups(pair):
+            return slice(SIDE * pair, SIDE * (pair + 1))
+
+        def load_w1(pair):
+            w1_raw[pair] = sbuf("w1_raw%d" % pair, [P, PACK, K], F32)
+            w1_bf[pair] = sbuf("w1_bf%d" % pair, [P, PACK * K], BF16)
+            nc.sync.dma_start(out=w1_raw[pair][:], in_=w1[groups(pair)].rearrange("g (p j) k -> (g p) j k", j=PACK))
+
+        def load_x(pair, first, count):
+            raw = sbuf("x_raw%d_%d" % (pair, first), [P, PACK, count * CH], F32)
+            rows = x[groups(pair)].rearrange("g (p j) n -> (g p) j n", j=PACK)
+            nc.sync.dma_start(out=raw[:], in_=rows[:, :, first * CH:(first + count) * CH])
+            for c in range(count):
+                x_raw[CHUNKS * pair + first + c] = (raw, c)
+
+        def load_hs():
+            nc.sync.dma_start(out=hs_sb[:, :, 0:PACK], in_=hs.rearrange("g (s t) o -> s g (t o)", t=PACK))
+
+        def load_w2(pair):
+            w2_raw[pair] = sbuf("w2_raw%d" % pair, [P, SIDE, PACK * M], F32)
+            nc.sync.dma_start(out=w2_raw[pair][:], in_=w2[groups(pair)].rearrange("g (s t) m -> s g (t m)", t=PACK))
+
+        def load_r(pair):
+            r_sb[pair] = sbuf("r_sb%d" % pair, [P, SIDE, N], F32)
+            res[pair] = sbuf("res%d" % pair, [P, SIDE, N], F32)
+            nc.sync.dma_start(out=r_sb[pair][:], in_=r[groups(pair)].rearrange("g m n -> m g n"))
+
+        def cast_w1(engine, pair, lo, hi):
+            dst = w1_bf[pair][:].rearrange("p (t s j) -> p s j t", t=PACK, j=PACK)
+            src = w1_raw[pair][:].rearrange("p j (s t) -> p s j t", t=PACK)
+            copy_on(engine, dst[:, lo:hi], src[:, lo:hi])
+
+        def quant_w1(pair):
+            w1_q[pair] = quantize("w1_%d" % pair, w1_bf[pair][:], K)
+
+        def cast_x(engine, step, count=1):
+            if step % 2 == 0:
+                x_bf[step // 2] = sbuf("x_bf%d" % step, [P, 2 * PACK * CH], BF16)
+            lo = (step % 2) * PACK * CH
+            dst = x_bf[step // 2][:, lo:lo + count * PACK * CH].rearrange("p (a e j) -> p a j e", e=2, j=PACK)
+            raw, first = x_raw[step]
+            copy_on(engine, dst, raw[:, :, first * CH:(first + count) * CH].rearrange("p j (a e) -> p a j e", e=2))
+
+        def quant_x(step, count=1):
+            lo = (step % 2) * PACK * CH
+            codes, scales = quantize("x_%d" % step, x_bf[step // 2][:, lo:lo + count * PACK * CH], count * CH)
+            for c in range(count):
+                x_q[step + c] = (codes[:, c * CH:(c + 1) * CH], scales[:, c * CH:(c + 1) * CH])
+
+        def cast_w2(engine, pair):
+            w2_bf[pair] = sbuf("w2_bf%d" % pair, [P, SIDE * PACK * M], BF16)
+            dst = w2_bf[pair][:].rearrange("p (g a e t) -> p g a t e", g=SIDE, e=2, t=PACK)
+            copy_on(engine, dst, w2_raw[pair][:].rearrange("p g (t a e) -> p g a t e", t=PACK, e=2))
+
+        def quant_w2(pair):
+            w2_q[pair] = quantize("w2_%d" % pair, w2_bf[pair][:], SIDE * M)
+
+        def first_layer(step):
+            w_codes, w_scales = w1_q[step // CHUNKS]
+            x_codes, x_scales = x_q[step]
+            for t in range(PACK):
+                cols = slice(t * P, (t + 1) * P)
+                for c in range(SIDE):
+                    rows = slice(ROWS * c, ROWS * (c + 1))
+                    nc.tensor.matmul_mx(out=z_banks[c][step % 2][:, t * CH:(t + 1) * CH],
+                                        lhsT=w_codes[rows, cols].bitcast(FP8X4), lhsT_scale=w_scales[rows, cols],
+                                        rhs=x_codes[rows, :].bitcast(FP8X4), rhs_scale=x_scales[rows, :],
+                                        start=True, stop=True)
+
+        def gelu(step, c):
+            if c == 0:
+                act[step] = sbuf("act%d" % step, [P, SIDE * CH * PACK], F32)
+                if step % 2 == 0:
+                    h_bf[step // 2] = sbuf("h_bf%d" % step, [P, 2 * SIDE * CH * PACK], BF16)
+            dst = act[step][:, c * CH * PACK:(c + 1) * CH * PACK].rearrange("p (n t) -> p n t", t=PACK)
+            nc.scalar.activation(out=dst, in_=z_banks[c][step % 2][:].rearrange("p (t n) -> p n t", t=PACK),
+                                 func=ACT.Gelu_apprx_tanh)
+
+        def scale(step, lo, hi):
+            span = slice(lo * CH * PACK, hi * CH * PACK)
+            g0 = SIDE * (step // CHUNKS)
+            factors = hs_sb[:, g0 + lo:g0 + hi, 0:PACK].unsqueeze(2).to_broadcast([P, hi - lo, CH, PACK])
+            at = (step % 2) * SIDE * CH * PACK
+            nc.vector.tensor_tensor(out=h_bf[step // 2][:, at + span.start:at + span.stop].rearrange("p (g n t) -> p g n t", n=CH, t=PACK),
+                                    in0=act[step][:, span].rearrange("p (g n t) -> p g n t", n=CH, t=PACK),
+                                    in1=factors, op=ALU.mult)
+
+        def quant_h(step, lo, hi):
+            at = (step % 2) * SIDE
+            codes, scales = quantize("h_%d_%d" % (step, lo), h_bf[step // 2][:, (at + lo) * CH * PACK:(at + hi) * CH * PACK], (hi - lo) * CH)
+            for u in range(lo, hi):
+                cols = slice((u - lo) * CH, (u - lo + 1) * CH)
+                h_q[step + u // SIDE, u % SIDE] = (codes[:, cols], scales[:, cols])
+
+        def second_layer(step, lo, hi):
+            w_codes, w_scales = w2_q[step // CHUNKS]
+            for c in range(lo, hi):
+                h_codes, h_scales = h_q[step, c]
+                cols = slice(c * M, (c + 1) * M)
+                nc.tensor.matmul_mx(out=y_banks[step // 2][:, (2 * c + step % 2) * CH:(2 * c + step % 2 + 1) * CH],
+                                    lhsT=w_codes[:, cols].bitcast(FP8X4), lhsT_scale=w_scales[:, cols],
+                                    rhs=h_codes.bitcast(FP8X4), rhs_scale=h_scales, start=True, stop=True)
+
+        def add(step, count, lo=0, hi=SIDE):
+            pair, chunk = divmod(step, CHUNKS)
+            cols = slice(chunk * CH, (chunk + count) * CH)
+            at = (step % 2) * CH
+            sums = y_banks[step // 2][:].rearrange("p (g n) -> p g n", g=SIDE)[:, lo:hi, at:at + count * CH]
+            nc.vector.tensor_tensor(out=res[pair][:, lo:hi, cols], in0=sums, in1=r_sb[pair][:, lo:hi, cols], op=ALU.add)
+
+        def store(pair, first, count, lo=0, hi=SIDE):
+            cols = slice(first * CH, (first + count) * CH)
+            nc.sync.dma_start(out=out[groups(pair)].rearrange("g m n -> m g n")[:, lo:hi, cols], in_=res[pair][:, lo:hi, cols])
+
+        def warm():
+            seed = sbuf("seed", [P, 8], F32)
+            spent = sbuf("spent", [P, 8], F32)
+            nc.gpsimd.memset(seed[:], 0.0)
+            nc.scalar.activation(out=spent[:], in_=seed[:], func=ACT.Gelu_apprx_tanh)
+
+        warm()
+        load_w1(0); load_x(0, 0, 1); load_x(0, 1, 1); load_hs(); load_x(0, 2, 2)
+        load_w2(0); load_w1(1); load_r(0); load_x(1, 0, 2); load_x(1, 2, 2); load_w2(1); load_r(1)
+        cast_w1("v", 0, 0, 88); cast_w1("s", 0, 88, 128)
+        cast_x("s", 0); quant_w1(0); quant_x(0); first_layer(0)
+        cast_x("s", 1); quant_x(1); first_layer(1); cast_x("v", 2, 2); gelu(0, 0); gelu(0, 1)
+        quant_x(2, 2); scale(0, 0, 1); scale(0, 1, 2); first_layer(2)
+        gelu(1, 0); gelu(1, 1); first_layer(3); cast_w2("v", 0); scale(1, 0, 2); quant_w2(0); quant_h(0, 0, 4)
+        second_layer(0, 0, 2); second_layer(1, 0, 2)
+        gelu(2, 0); gelu(2, 1); cast_w1("s", 1, 0, 128); scale(2, 0, 2)
+        cast_x("s", 4); quant_w1(1); quant_x(4); first_layer(4); add(0, 2); quant_h(2, 0, 2); second_layer(2, 0, 2)
+        gelu(3, 0); gelu(3, 1); cast_x("s", 5)
+        scale(3, 0, 2); quant_x(5); first_layer(5); quant_h(3, 0, 2); second_layer(3, 0, 2)
+        gelu(4, 0); gelu(4, 1); cast_x("s", 6)
+        scale(4, 0, 2); quant_x(6); first_layer(6); add(2, 2); store(0, 0, 4)
+        gelu(5, 0); gelu(5, 1); cast_x("s", 7)
+        scale(5, 0, 2); quant_x(7); first_layer(7); quant_h(4, 0, 4)
+        gelu(6, 0); gelu(6, 1); cast_w2("s", 1); scale(6, 0, 2); quant_w2(1); second_layer(4, 0, 2); second_layer(5, 0, 2)
+        quant_h(6, 0, 2); second_layer(6, 0, 2); add(4, 2); store(1, 0, 2)
+        gelu(7, 0); gelu(7, 1); scale(7, 0, 1); add(6, 1); store(1, 2, 1); quant_h(7, 0, 1); second_layer(7, 0, 1)
+        scale(7, 1, 2); add(7, 1, 0, 1); quant_h(7, 1, 2); second_layer(7, 1, 2); add(7, 1, 1, 2); store(1, 3, 1)

@@ -45,15 +45,15 @@ def tile_rows_gmlp_gelu_res_kernel(tc, x, w1, hs, w2, r, out):
             nc.vector.quantize_mx(out=codes[:].bitcast(FP8X4), scales=scales[:], in_=src)
             return codes, scales
 
-        z_banks = [[ps.tile([P, PACK * CH], F32, name="z%d_%d" % (c, b)) for b in range(2)] for c in range(SIDE)]
-        y_banks = [ps.tile([P, PACK * CH], F32, name="y%d" % b) for b in range(4)]
+        z_banks = [[ps.tile([P, PACK * CH], F32, name="z%d_%d" % (c, b)) for b in range(3)] for c in range(SIDE)]
+        y_banks = [ps.tile([P, PACK * CH], F32, name="y%d" % b) for b in range(2)]
 
         w1_raw, w1_bf, w1_q = {}, {}, {}
         x_raw, x_bf, x_q = {}, {}, {}
         w2_raw, w2_bf, w2_q = {}, {}, {}
         r_sb, res = {}, {}
         act, h_bf, h_q = {}, {}, {}
-        hs_sb = sbuf("hs_sb", [P, G, 8], F32)
+        hs_sb, h_own, flat = {}, {}, {}
 
         def groups(pair):
             return slice(SIDE * pair, SIDE * (pair + 1))
@@ -70,8 +70,12 @@ def tile_rows_gmlp_gelu_res_kernel(tc, x, w1, hs, w2, r, out):
             for c in range(count):
                 x_raw[CHUNKS * pair + first + c] = (raw, c)
 
-        def load_hs():
-            nc.sync.dma_start(out=hs_sb[:, :, 0:PACK], in_=hs.rearrange("g (s t) o -> s g (t o)", t=PACK))
+        def load_hs2(pair):
+            hs_sb[pair] = sbuf("hs_sb%d" % pair, [P, SIDE, 8], F32)
+            nc.sync.dma_start(out=hs_sb[pair][:, :, 0:PACK], in_=hs[groups(pair)].rearrange("g (s t) o -> s g (t o)", t=PACK))
+
+        def y_bank(step):
+            return 0 if step == STEPS - 1 else (step // 2) % 2
 
         def load_w2(pair):
             w2_raw[pair] = sbuf("w2_raw%d" % pair, [P, SIDE, PACK * M], F32)
@@ -115,28 +119,40 @@ def tile_rows_gmlp_gelu_res_kernel(tc, x, w1, hs, w2, r, out):
         def first_layer(step):
             w_codes, w_scales = w1_q[step // CHUNKS]
             x_codes, x_scales = x_q[step]
-            for t in range(PACK):
-                cols = slice(t * P, (t + 1) * P)
-                for c in range(SIDE):
-                    rows = slice(ROWS * c, ROWS * (c + 1))
-                    nc.tensor.matmul_mx(out=z_banks[c][step % 2][:, t * CH:(t + 1) * CH],
+            for c in range(SIDE):
+                rows = slice(ROWS * c, ROWS * (c + 1))
+                for t in range(PACK):
+                    cols = slice(t * P, (t + 1) * P)
+                    nc.tensor.matmul_mx(out=z_banks[c][step % 3][:, t * CH:(t + 1) * CH],
                                         lhsT=w_codes[rows, cols].bitcast(FP8X4), lhsT_scale=w_scales[rows, cols],
                                         rhs=x_codes[rows, :].bitcast(FP8X4), rhs_scale=x_scales[rows, :],
                                         start=True, stop=True)
 
         def gelu(step, c):
-            if c == 0:
+            if step not in act:
                 act[step] = sbuf("act%d" % step, [P, SIDE * CH * PACK], F32)
                 if step % 2 == 0:
                     h_bf[step // 2] = sbuf("h_bf%d" % step, [P, 2 * SIDE * CH * PACK], BF16)
             dst = act[step][:, c * CH * PACK:(c + 1) * CH * PACK].rearrange("p (n t) -> p n t", t=PACK)
-            nc.scalar.activation(out=dst, in_=z_banks[c][step % 2][:].rearrange("p (t n) -> p n t", t=PACK),
+            nc.scalar.activation(out=dst, in_=z_banks[c][step % 3][:].rearrange("p (t n) -> p n t", t=PACK),
                                  func=ACT.Gelu_apprx_tanh)
+
+        def gelu_flat(step, c):
+            flat[step, c] = sbuf("flat%d_%d" % (step, c), [P, PACK * CH], F32)
+            nc.scalar.activation(out=flat[step, c][:], in_=z_banks[c][step % 3][:], func=ACT.Gelu_apprx_tanh)
+
+        def scale_s(step, c):
+            rounded = sbuf("rounded%d_%d" % (step, c), [P, PACK * CH], BF16)
+            for t in range(PACK):
+                nc.scalar.activation(out=rounded[:, t * CH:(t + 1) * CH], in_=flat[step, c][:, t * CH:(t + 1) * CH],
+                                     func=ACT.Copy, scale=hs_sb[step // CHUNKS][:, c, t:t + 1])
+            h_own[step, c] = sbuf("h_own%d_%d" % (step, c), [P, PACK * CH], BF16)
+            nc.scalar.copy(out=h_own[step, c][:].rearrange("p (a e t) -> p a t e", e=4, t=PACK),
+                           in_=rounded[:].rearrange("p (t a e) -> p a t e", e=4, t=PACK))
 
         def scale(step, lo, hi):
             span = slice(lo * CH * PACK, hi * CH * PACK)
-            g0 = SIDE * (step // CHUNKS)
-            factors = hs_sb[:, g0 + lo:g0 + hi, 0:PACK].unsqueeze(2).to_broadcast([P, hi - lo, CH, PACK])
+            factors = hs_sb[step // CHUNKS][:, lo:hi, 0:PACK].unsqueeze(2).to_broadcast([P, hi - lo, CH, PACK])
             at = (step % 2) * SIDE * CH * PACK
             nc.vector.tensor_tensor(out=h_bf[step // 2][:, at + span.start:at + span.stop].rearrange("p (g n t) -> p g n t", n=CH, t=PACK),
                                     in0=act[step][:, span].rearrange("p (g n t) -> p g n t", n=CH, t=PACK),
@@ -144,7 +160,8 @@ def tile_rows_gmlp_gelu_res_kernel(tc, x, w1, hs, w2, r, out):
 
         def quant_h(step, lo, hi):
             at = (step % 2) * SIDE
-            codes, scales = quantize("h_%d_%d" % (step, lo), h_bf[step // 2][:, (at + lo) * CH * PACK:(at + hi) * CH * PACK], (hi - lo) * CH)
+            src = h_own[step, lo][:] if (step, lo) in h_own else h_bf[step // 2][:, (at + lo) * CH * PACK:(at + hi) * CH * PACK]
+            codes, scales = quantize("h_%d_%d" % (step, lo), src, (hi - lo) * CH)
             for u in range(lo, hi):
                 cols = slice((u - lo) * CH, (u - lo + 1) * CH)
                 h_q[step + u // SIDE, u % SIDE] = (codes[:, cols], scales[:, cols])
@@ -154,7 +171,7 @@ def tile_rows_gmlp_gelu_res_kernel(tc, x, w1, hs, w2, r, out):
             for c in range(lo, hi):
                 h_codes, h_scales = h_q[step, c]
                 cols = slice(c * M, (c + 1) * M)
-                nc.tensor.matmul_mx(out=y_banks[step // 2][:, (2 * c + step % 2) * CH:(2 * c + step % 2 + 1) * CH],
+                nc.tensor.matmul_mx(out=y_banks[y_bank(step)][:, (2 * c + step % 2) * CH:(2 * c + step % 2 + 1) * CH],
                                     lhsT=w_codes[:, cols].bitcast(FP8X4), lhsT_scale=w_scales[:, cols],
                                     rhs=h_codes.bitcast(FP8X4), rhs_scale=h_scales, start=True, stop=True)
 
@@ -162,7 +179,7 @@ def tile_rows_gmlp_gelu_res_kernel(tc, x, w1, hs, w2, r, out):
             pair, chunk = divmod(step, CHUNKS)
             cols = slice(chunk * CH, (chunk + count) * CH)
             at = (step % 2) * CH
-            sums = y_banks[step // 2][:].rearrange("p (g n) -> p g n", g=SIDE)[:, lo:hi, at:at + count * CH]
+            sums = y_banks[y_bank(step)][:].rearrange("p (g n) -> p g n", g=SIDE)[:, lo:hi, at:at + count * CH]
             nc.vector.tensor_tensor(out=res[pair][:, lo:hi, cols], in0=sums, in1=r_sb[pair][:, lo:hi, cols], op=ALU.add)
 
         def store(pair, first, count, lo=0, hi=SIDE):
@@ -176,23 +193,40 @@ def tile_rows_gmlp_gelu_res_kernel(tc, x, w1, hs, w2, r, out):
             nc.scalar.activation(out=spent[:], in_=seed[:], func=ACT.Gelu_apprx_tanh)
 
         warm()
-        load_w1(0); load_x(0, 0, 1); load_x(0, 1, 1); load_hs(); load_x(0, 2, 2)
-        load_w2(0); load_w1(1); load_r(0); load_x(1, 0, 2); load_x(1, 2, 2); load_w2(1); load_r(1)
+        load_w1(0); load_x(0, 0, 1); load_hs2(0); load_x(0, 1, 1); load_x(0, 2, 2)
+        load_w2(0); load_w1(1); load_x(1, 0, 2); load_r(0); load_hs2(1); load_x(1, 2, 2); load_w2(1); load_r(1)
         cast_w1("v", 0, 0, 88); cast_w1("s", 0, 88, 128)
         cast_x("s", 0); quant_w1(0); quant_x(0); first_layer(0)
-        cast_x("s", 1); quant_x(1); first_layer(1); cast_x("v", 2, 2); gelu(0, 0); gelu(0, 1)
-        quant_x(2, 2); scale(0, 0, 1); scale(0, 1, 2); first_layer(2)
-        gelu(1, 0); gelu(1, 1); first_layer(3); cast_w2("v", 0); scale(1, 0, 2); quant_w2(0); quant_h(0, 0, 4)
-        second_layer(0, 0, 2); second_layer(1, 0, 2)
-        gelu(2, 0); gelu(2, 1); cast_w1("s", 1, 0, 128); scale(2, 0, 2)
-        cast_x("s", 4); quant_w1(1); quant_x(4); first_layer(4); add(0, 2); quant_h(2, 0, 2); second_layer(2, 0, 2)
-        gelu(3, 0); gelu(3, 1); cast_x("s", 5)
-        scale(3, 0, 2); quant_x(5); first_layer(5); quant_h(3, 0, 2); second_layer(3, 0, 2)
-        gelu(4, 0); gelu(4, 1); cast_x("s", 6)
-        scale(4, 0, 2); quant_x(6); first_layer(6); add(2, 2); store(0, 0, 4)
-        gelu(5, 0); gelu(5, 1); cast_x("s", 7)
-        scale(5, 0, 2); quant_x(7); first_layer(7); quant_h(4, 0, 4)
-        gelu(6, 0); gelu(6, 1); cast_w2("s", 1); scale(6, 0, 2); quant_w2(1); second_layer(4, 0, 2); second_layer(5, 0, 2)
-        quant_h(6, 0, 2); second_layer(6, 0, 2); add(4, 2); store(1, 0, 2)
-        gelu(7, 0); gelu(7, 1); scale(7, 0, 1); add(6, 1); store(1, 2, 1); quant_h(7, 0, 1); second_layer(7, 0, 1)
-        scale(7, 1, 2); add(7, 1, 0, 1); quant_h(7, 1, 2); second_layer(7, 1, 2); add(7, 1, 1, 2); store(1, 3, 1)
+        cast_x("s", 1); quant_x(1); first_layer(1); cast_x("v", 2, 2)
+        gelu(0, 0); gelu(0, 1)
+        scale(0, 0, 1); quant_x(2, 2); first_layer(2); first_layer(3); scale(0, 1, 2); cast_w2("v", 0)
+        gelu(1, 0); gelu(1, 1)
+        scale(1, 0, 2)
+        quant_w2(0); quant_h(0, 0, 4); second_layer(0, 0, 2); second_layer(1, 0, 2)
+        gelu(2, 0); gelu(2, 1)
+        cast_w1("s", 1, 16, 128)
+        cast_x("s", 4)
+        cast_w1("v", 1, 0, 16)
+        scale(2, 0, 2)
+        quant_w1(1)
+        quant_x(4); first_layer(4)
+        add(0, 2)
+        gelu(3, 0); gelu(3, 1)
+        cast_x("s", 5)
+        scale(3, 0, 2)
+        quant_x(5); first_layer(5)
+        quant_h(2, 0, 4); second_layer(2, 0, 2); second_layer(3, 0, 2)
+        gelu(4, 0); gelu(4, 1)
+        cast_x("s", 6)
+        scale(4, 0, 2)
+        quant_x(6); first_layer(6)
+        add(2, 2); store(0, 0, 4)
+        gelu(5, 0); gelu(5, 1)
+        cast_x("s", 7)
+        cast_w2("s", 1)
+        scale(5, 0, 2)
+        quant_x(7); first_layer(7)
+        quant_w2(1); quant_h(4, 0, 4); second_layer(4, 0, 2); second_layer(5, 0, 2)
+        gelu(6, 1); gelu_flat(6, 0); gelu(7, 0); gelu(7, 1); scale_s(6, 0)
+        scale(6, 1, 2); scale(7, 0, 1); scale(7, 1, 2); add(4, 2); store(1, 0, 2); quant_h(7, 0, 2); second_layer(7, 0, 2); quant_h(6, 1, 2); second_layer(6, 1, 2)
+        quant_h(6, 0, 1); second_layer(6, 0, 1); add(7, 1); store(1, 3, 1); add(6, 1); store(1, 2, 1)

@@ -17,10 +17,14 @@ P = 128
 PACK = 4
 ROWS = D // PACK
 SIDE = P // ROWS
-PAIRS = G // SIDE
 CH = 128
 CHUNKS = N // CH
-STEPS = PAIRS * CHUNKS
+STEPS = G // SIDE * CHUNKS
+UNIT = PACK * CH
+Z_BANKS = 3
+AHEAD = 2
+HS_ROW = 8
+W1_ON_VECTOR = (76, 36)
 
 
 def tile_rows_gmlp_gelu_res_kernel(tc, x, w1, hs, w2, r, out):
@@ -33,200 +37,227 @@ def tile_rows_gmlp_gelu_res_kernel(tc, x, w1, hs, w2, r, out):
         def sbuf(name, shape, dtype):
             return sb.tile(shape, dtype, name=name, align_bytes=64)
 
-        def copy_on(engine, dst, src):
-            if engine == "v":
-                nc.vector.tensor_copy(out=dst, in_=src)
-            else:
-                nc.scalar.copy(out=dst, in_=src)
-
-        def quantize(name, src, words):
+        def quantize(name, values, words):
             codes = sbuf(name + "_codes", [P, words], U32)
             scales = sbuf(name + "_scales", [P, words], U8)
-            nc.vector.quantize_mx(out=codes[:].bitcast(FP8X4), scales=scales[:], in_=src)
+            nc.vector.quantize_mx(out=codes[:].bitcast(FP8X4), scales=scales[:], in_=values)
             return codes, scales
 
-        z_banks = [[ps.tile([P, PACK * CH], F32, name="z%d_%d" % (c, b)) for b in range(3)] for c in range(SIDE)]
-        y_banks = [ps.tile([P, PACK * CH], F32, name="y%d" % b) for b in range(2)]
+        def multiply(sums, weights, moving, partitions, columns):
+            nc.tensor.matmul_mx(
+                out=sums,
+                lhsT=weights[0][partitions, columns].bitcast(FP8X4),
+                lhsT_scale=weights[1][partitions, columns],
+                rhs=moving[0][partitions, :].bitcast(FP8X4),
+                rhs_scale=moving[1][partitions, :],
+                start=True,
+                stop=True,
+            )
 
-        w1_raw, w1_bf, w1_q = {}, {}, {}
-        x_raw, x_bf, x_q = {}, {}, {}
-        w2_raw, w2_bf, w2_q = {}, {}, {}
-        r_sb, res = {}, {}
-        act, h_bf, h_q = {}, {}, {}
-        hs_sb, h_own, flat = {}, {}, {}
+        on_vector, on_scalar = nc.vector.tensor_copy, nc.scalar.copy
+
+        z_banks = [[ps.tile([P, UNIT], F32, name="z%d_%d" % (c, b)) for b in range(Z_BANKS)] for c in range(SIDE)]
+        y_banks = [ps.tile([P, SIDE * 2 * CH], F32, name="y%d" % b) for b in range(2)]
+
+        w1_raw, w1_bf, w1_mx = {}, {}, {}
+        x_raw, x_bf, x_mx = {}, {}, {}
+        w2_raw, w2_bf, w2_mx = {}, {}, {}
+        hs_sb, r_sb, result = {}, {}, {}
+        act, h_bf, h_mx = {}, {}, {}
 
         def groups(pair):
             return slice(SIDE * pair, SIDE * (pair + 1))
 
+        def y_bank(step):
+            turn = step // 2 + (step == STEPS - 1)
+            return y_banks[turn % 2][:].rearrange("p (c n) -> p c n", c=SIDE)
+
         def load_w1(pair):
             w1_raw[pair] = sbuf("w1_raw%d" % pair, [P, PACK, K], F32)
             w1_bf[pair] = sbuf("w1_bf%d" % pair, [P, PACK * K], BF16)
-            nc.sync.dma_start(out=w1_raw[pair][:], in_=w1[groups(pair)].rearrange("g (p j) k -> (g p) j k", j=PACK))
+            nc.sync.dma_start(out=w1_raw[pair][:], in_=w1[groups(pair)].rearrange("c (p j) k -> (c p) j k", j=PACK))
 
-        def load_x(pair, first, count):
-            raw = sbuf("x_raw%d_%d" % (pair, first), [P, PACK, count * CH], F32)
-            rows = x[groups(pair)].rearrange("g (p j) n -> (g p) j n", j=PACK)
-            nc.sync.dma_start(out=raw[:], in_=rows[:, :, first * CH:(first + count) * CH])
-            for c in range(count):
-                x_raw[CHUNKS * pair + first + c] = (raw, c)
+        def load_x(step, count):
+            pair, chunk = divmod(step, CHUNKS)
+            raw = sbuf("x_raw%d" % step, [P, PACK, count * CH], F32)
+            rows = x[groups(pair)].rearrange("c (p j) n -> (c p) j n", j=PACK)
+            nc.sync.dma_start(out=raw[:], in_=rows[:, :, chunk * CH:(chunk + count) * CH])
+            for i in range(count):
+                x_raw[step + i] = (raw, i * CH)
 
-        def load_hs2(pair):
-            hs_sb[pair] = sbuf("hs_sb%d" % pair, [P, SIDE, 8], F32)
-            nc.sync.dma_start(out=hs_sb[pair][:, :, 0:PACK], in_=hs[groups(pair)].rearrange("g (s t) o -> s g (t o)", t=PACK))
-
-        def y_bank(step):
-            return 0 if step == STEPS - 1 else (step // 2) % 2
+        def load_hs(pair):
+            hs_sb[pair] = sbuf("hs%d" % pair, [P, SIDE, HS_ROW], F32)
+            nc.sync.dma_start(out=hs_sb[pair][:, :, 0:PACK], in_=hs[groups(pair)].rearrange("c (s t) o -> s c (t o)", t=PACK))
 
         def load_w2(pair):
             w2_raw[pair] = sbuf("w2_raw%d" % pair, [P, SIDE, PACK * M], F32)
-            nc.sync.dma_start(out=w2_raw[pair][:], in_=w2[groups(pair)].rearrange("g (s t) m -> s g (t m)", t=PACK))
+            nc.sync.dma_start(out=w2_raw[pair][:], in_=w2[groups(pair)].rearrange("c (s t) m -> s c (t m)", t=PACK))
 
         def load_r(pair):
-            r_sb[pair] = sbuf("r_sb%d" % pair, [P, SIDE, N], F32)
-            res[pair] = sbuf("res%d" % pair, [P, SIDE, N], F32)
-            nc.sync.dma_start(out=r_sb[pair][:], in_=r[groups(pair)].rearrange("g m n -> m g n"))
+            r_sb[pair] = sbuf("r%d" % pair, [P, SIDE, N], F32)
+            result[pair] = sbuf("result%d" % pair, [P, SIDE, N], F32)
+            nc.sync.dma_start(out=r_sb[pair][:], in_=r[groups(pair)].rearrange("c m n -> m c n"))
 
-        def cast_w1(engine, pair, lo, hi):
-            dst = w1_bf[pair][:].rearrange("p (t s j) -> p s j t", t=PACK, j=PACK)
-            src = w1_raw[pair][:].rearrange("p j (s t) -> p s j t", t=PACK)
-            copy_on(engine, dst[:, lo:hi], src[:, lo:hi])
+        def store(step, count):
+            pair, chunk = divmod(step, CHUNKS)
+            cols = slice(chunk * CH, (chunk + count) * CH)
+            nc.sync.dma_start(out=out[groups(pair)].rearrange("c m n -> m c n")[:, :, cols], in_=result[pair][:, :, cols])
 
-        def quant_w1(pair):
-            w1_q[pair] = quantize("w1_%d" % pair, w1_bf[pair][:], K)
+        def round_w1(copy, pair, lo, hi):
+            dealt = w1_bf[pair][:].rearrange("p (t s j) -> p s j t", t=PACK, j=PACK)
+            raw = w1_raw[pair][:].rearrange("p j (s t) -> p s j t", t=PACK)
+            copy(out=dealt[:, lo:hi], in_=raw[:, lo:hi])
 
-        def cast_x(engine, step, count=1):
+        def round_x(copy, step, count=1):
             if step % 2 == 0:
-                x_bf[step // 2] = sbuf("x_bf%d" % step, [P, 2 * PACK * CH], BF16)
-            lo = (step % 2) * PACK * CH
-            dst = x_bf[step // 2][:, lo:lo + count * PACK * CH].rearrange("p (a e j) -> p a j e", e=2, j=PACK)
+                x_bf[step // 2] = sbuf("x_bf%d" % step, [P, 2 * UNIT], BF16)
+            at = step % 2 * UNIT
             raw, first = x_raw[step]
-            copy_on(engine, dst, raw[:, :, first * CH:(first + count) * CH].rearrange("p j (a e) -> p a j e", e=2))
+            copy(out=x_bf[step // 2][:, at:at + count * UNIT].rearrange("p (a e j) -> p a j e", e=2, j=PACK),
+                 in_=raw[:, :, first:first + count * CH].rearrange("p j (a e) -> p a j e", e=2))
 
-        def quant_x(step, count=1):
-            lo = (step % 2) * PACK * CH
-            codes, scales = quantize("x_%d" % step, x_bf[step // 2][:, lo:lo + count * PACK * CH], count * CH)
-            for c in range(count):
-                x_q[step + c] = (codes[:, c * CH:(c + 1) * CH], scales[:, c * CH:(c + 1) * CH])
-
-        def cast_w2(engine, pair):
+        def round_w2(copy, pair):
             w2_bf[pair] = sbuf("w2_bf%d" % pair, [P, SIDE * PACK * M], BF16)
-            dst = w2_bf[pair][:].rearrange("p (g a e t) -> p g a t e", g=SIDE, e=2, t=PACK)
-            copy_on(engine, dst, w2_raw[pair][:].rearrange("p g (t a e) -> p g a t e", t=PACK, e=2))
+            copy(out=w2_bf[pair][:].rearrange("p (c a e t) -> p c a t e", c=SIDE, e=2, t=PACK),
+                 in_=w2_raw[pair][:].rearrange("p c (t a e) -> p c a t e", t=PACK, e=2))
 
-        def quant_w2(pair):
-            w2_q[pair] = quantize("w2_%d" % pair, w2_bf[pair][:], SIDE * M)
+        def quantize_w1(pair):
+            w1_mx[pair] = quantize("w1_%d" % pair, w1_bf[pair][:], K)
+
+        def quantize_w2(pair):
+            w2_mx[pair] = quantize("w2_%d" % pair, w2_bf[pair][:], SIDE * M)
+
+        def quantize_x(step, count=1):
+            at = step % 2 * UNIT
+            codes, scales = quantize("x_%d" % step, x_bf[step // 2][:, at:at + count * UNIT], count * CH)
+            for i in range(count):
+                x_mx[step + i] = (codes[:, i * CH:(i + 1) * CH], scales[:, i * CH:(i + 1) * CH])
 
         def first_layer(step):
-            w_codes, w_scales = w1_q[step // CHUNKS]
-            x_codes, x_scales = x_q[step]
-            for c in range(SIDE):
-                rows = slice(ROWS * c, ROWS * (c + 1))
-                for t in range(PACK):
-                    cols = slice(t * P, (t + 1) * P)
-                    nc.tensor.matmul_mx(out=z_banks[c][step % 3][:, t * CH:(t + 1) * CH],
-                                        lhsT=w_codes[rows, cols].bitcast(FP8X4), lhsT_scale=w_scales[rows, cols],
-                                        rhs=x_codes[rows, :].bitcast(FP8X4), rhs_scale=x_scales[rows, :],
-                                        start=True, stop=True)
+            for t in range(PACK):
+                for c in range(SIDE):
+                    multiply(z_banks[c][step % Z_BANKS][:, t * CH:(t + 1) * CH], w1_mx[step // CHUNKS], x_mx[step],
+                             slice(ROWS * c, ROWS * (c + 1)), slice(t * P, (t + 1) * P))
 
         def gelu(step, c):
             if step not in act:
-                act[step] = sbuf("act%d" % step, [P, SIDE * CH * PACK], F32)
+                act[step] = sbuf("act%d" % step, [P, SIDE * UNIT], F32)
                 if step % 2 == 0:
-                    h_bf[step // 2] = sbuf("h_bf%d" % step, [P, 2 * SIDE * CH * PACK], BF16)
-            dst = act[step][:, c * CH * PACK:(c + 1) * CH * PACK].rearrange("p (n t) -> p n t", t=PACK)
-            nc.scalar.activation(out=dst, in_=z_banks[c][step % 3][:].rearrange("p (t n) -> p n t", t=PACK),
+                    h_bf[step // 2] = sbuf("h_bf%d" % step, [P, 2 * SIDE * UNIT], BF16)
+            nc.scalar.activation(out=act[step][:, c * UNIT:(c + 1) * UNIT].rearrange("p (n t) -> p n t", t=PACK),
+                                 in_=z_banks[c][step % Z_BANKS][:].rearrange("p (t n) -> p n t", t=PACK),
                                  func=ACT.Gelu_apprx_tanh)
 
-        def gelu_flat(step, c):
-            flat[step, c] = sbuf("flat%d_%d" % (step, c), [P, PACK * CH], F32)
-            nc.scalar.activation(out=flat[step, c][:], in_=z_banks[c][step % 3][:], func=ACT.Gelu_apprx_tanh)
+        def h_values(step, lo, hi):
+            at = step % 2 * SIDE
+            return h_bf[step // 2][:, (at + lo) * UNIT:(at + hi) * UNIT]
 
-        def scale_s(step, c):
-            rounded = sbuf("rounded%d_%d" % (step, c), [P, PACK * CH], BF16)
-            for t in range(PACK):
-                nc.scalar.activation(out=rounded[:, t * CH:(t + 1) * CH], in_=flat[step, c][:, t * CH:(t + 1) * CH],
-                                     func=ACT.Copy, scale=hs_sb[step // CHUNKS][:, c, t:t + 1])
-            h_own[step, c] = sbuf("h_own%d_%d" % (step, c), [P, PACK * CH], BF16)
-            nc.scalar.copy(out=h_own[step, c][:].rearrange("p (a e t) -> p a t e", e=4, t=PACK),
-                           in_=rounded[:].rearrange("p (t a e) -> p a t e", e=4, t=PACK))
-
-        def scale(step, lo, hi):
-            span = slice(lo * CH * PACK, hi * CH * PACK)
+        def scale(step, lo=0, hi=SIDE):
             factors = hs_sb[step // CHUNKS][:, lo:hi, 0:PACK].unsqueeze(2).to_broadcast([P, hi - lo, CH, PACK])
-            at = (step % 2) * SIDE * CH * PACK
-            nc.vector.tensor_tensor(out=h_bf[step // 2][:, at + span.start:at + span.stop].rearrange("p (g n t) -> p g n t", n=CH, t=PACK),
-                                    in0=act[step][:, span].rearrange("p (g n t) -> p g n t", n=CH, t=PACK),
+            nc.vector.tensor_tensor(out=h_values(step, lo, hi).rearrange("p (c n t) -> p c n t", n=CH, t=PACK),
+                                    in0=act[step][:, lo * UNIT:hi * UNIT].rearrange("p (c n t) -> p c n t", n=CH, t=PACK),
                                     in1=factors, op=ALU.mult)
 
-        def quant_h(step, lo, hi):
-            at = (step % 2) * SIDE
-            src = h_own[step, lo][:] if (step, lo) in h_own else h_bf[step // 2][:, (at + lo) * CH * PACK:(at + hi) * CH * PACK]
-            codes, scales = quantize("h_%d_%d" % (step, lo), src, (hi - lo) * CH)
+        def quantize_h(step, lo, hi):
+            codes, scales = quantize("h_%d_%d" % (step, lo), h_values(step, lo, hi), (hi - lo) * CH)
             for u in range(lo, hi):
                 cols = slice((u - lo) * CH, (u - lo + 1) * CH)
-                h_q[step + u // SIDE, u % SIDE] = (codes[:, cols], scales[:, cols])
+                h_mx[step + u // SIDE, u % SIDE] = (codes[:, cols], scales[:, cols])
 
-        def second_layer(step, lo, hi):
-            w_codes, w_scales = w2_q[step // CHUNKS]
+        def second_layer(step, lo=0, hi=SIDE):
+            at = step % 2 * CH
             for c in range(lo, hi):
-                h_codes, h_scales = h_q[step, c]
-                cols = slice(c * M, (c + 1) * M)
-                nc.tensor.matmul_mx(out=y_banks[y_bank(step)][:, (2 * c + step % 2) * CH:(2 * c + step % 2 + 1) * CH],
-                                    lhsT=w_codes[:, cols].bitcast(FP8X4), lhsT_scale=w_scales[:, cols],
-                                    rhs=h_codes.bitcast(FP8X4), rhs_scale=h_scales, start=True, stop=True)
+                multiply(y_bank(step)[:, c, at:at + CH], w2_mx[step // CHUNKS], h_mx[step, c],
+                         slice(0, P), slice(c * M, (c + 1) * M))
 
-        def add(step, count, lo=0, hi=SIDE):
+        def add_residual(step, count):
             pair, chunk = divmod(step, CHUNKS)
             cols = slice(chunk * CH, (chunk + count) * CH)
-            at = (step % 2) * CH
-            sums = y_banks[y_bank(step)][:].rearrange("p (g n) -> p g n", g=SIDE)[:, lo:hi, at:at + count * CH]
-            nc.vector.tensor_tensor(out=res[pair][:, lo:hi, cols], in0=sums, in1=r_sb[pair][:, lo:hi, cols], op=ALU.add)
+            at = step % 2 * CH
+            nc.vector.tensor_tensor(out=result[pair][:, :, cols], in0=y_bank(step)[:, :, at:at + count * CH],
+                                    in1=r_sb[pair][:, :, cols], op=ALU.add)
 
-        def store(pair, first, count, lo=0, hi=SIDE):
-            cols = slice(first * CH, (first + count) * CH)
-            nc.sync.dma_start(out=out[groups(pair)].rearrange("g m n -> m g n")[:, lo:hi, cols], in_=res[pair][:, lo:hi, cols])
+        load_w1(0)
+        load_x(0, 1)
+        load_x(1, 1)
+        load_x(2, 2)
+        load_hs(0)
+        load_w2(0)
+        load_w1(1)
+        load_x(4, 2)
+        load_r(0)
+        load_hs(1)
+        load_x(6, 2)
+        load_w2(1)
+        load_r(1)
 
-        def warm():
-            seed = sbuf("seed", [P, 8], F32)
-            spent = sbuf("spent", [P, 8], F32)
-            nc.gpsimd.memset(seed[:], 0.0)
-            nc.scalar.activation(out=spent[:], in_=seed[:], func=ACT.Gelu_apprx_tanh)
+        round_w1(on_vector, 0, 0, W1_ON_VECTOR[0])
+        round_w1(on_scalar, 0, W1_ON_VECTOR[0], P)
+        round_x(on_vector, 0)
+        quantize_w1(0)
+        quantize_x(0)
+        first_layer(0)
+        round_x(on_vector, 1)
+        quantize_x(1)
+        first_layer(1)
+        round_x(on_vector, 2, 2)
 
-        warm()
-        load_w1(0); load_x(0, 0, 1); load_hs2(0); load_x(0, 1, 1); load_x(0, 2, 2)
-        load_w2(0); load_w1(1); load_x(1, 0, 2); load_r(0); load_hs2(1); load_x(1, 2, 2); load_w2(1); load_r(1)
-        cast_w1("v", 0, 0, 88); cast_w1("s", 0, 88, 128)
-        cast_x("s", 0); quant_w1(0); quant_x(0); first_layer(0)
-        cast_x("s", 1); quant_x(1); first_layer(1); cast_x("v", 2, 2)
-        gelu(0, 0); gelu(0, 1)
-        scale(0, 0, 1); quant_x(2, 2); first_layer(2); first_layer(3); scale(0, 1, 2); cast_w2("v", 0)
-        gelu(1, 0); gelu(1, 1)
-        scale(1, 0, 2)
-        quant_w2(0); quant_h(0, 0, 4); second_layer(0, 0, 2); second_layer(1, 0, 2)
-        gelu(2, 0); gelu(2, 1)
-        cast_w1("s", 1, 16, 128)
-        cast_x("s", 4)
-        cast_w1("v", 1, 0, 16)
-        scale(2, 0, 2)
-        quant_w1(1)
-        quant_x(4); first_layer(4)
-        add(0, 2)
-        gelu(3, 0); gelu(3, 1)
-        cast_x("s", 5)
-        scale(3, 0, 2)
-        quant_x(5); first_layer(5)
-        quant_h(2, 0, 4); second_layer(2, 0, 2); second_layer(3, 0, 2)
-        gelu(4, 0); gelu(4, 1)
-        cast_x("s", 6)
-        scale(4, 0, 2)
-        quant_x(6); first_layer(6)
-        add(2, 2); store(0, 0, 4)
-        gelu(5, 0); gelu(5, 1)
-        cast_x("s", 7)
-        cast_w2("s", 1)
-        scale(5, 0, 2)
-        quant_x(7); first_layer(7)
-        quant_w2(1); quant_h(4, 0, 4); second_layer(4, 0, 2); second_layer(5, 0, 2)
-        gelu(6, 1); gelu_flat(6, 0); gelu(7, 0); gelu(7, 1); scale_s(6, 0)
-        scale(6, 1, 2); scale(7, 0, 1); scale(7, 1, 2); add(4, 2); store(1, 0, 2); quant_h(7, 0, 2); second_layer(7, 0, 2); quant_h(6, 1, 2); second_layer(6, 1, 2)
-        quant_h(6, 0, 1); second_layer(6, 0, 1); add(7, 1); store(1, 3, 1); add(6, 1); store(1, 2, 1)
+        gelu(0, 0)
+        gelu(0, 1)
+        scale(0, 0, 1)
+        quantize_x(2, 2)
+        first_layer(2)
+        first_layer(3)
+        scale(0, 1, 2)
+        round_w2(on_vector, 0)
+
+        last = STEPS - 1
+        for step in range(1, last - 1):
+            ahead = step + AHEAD
+            opens_pair = ahead == CHUNKS
+            gelu(step, 0)
+            gelu(step, 1)
+            if opens_pair:
+                round_w1(on_scalar, 1, W1_ON_VECTOR[1], P)
+            if ahead >= CHUNKS:
+                round_x(on_scalar, ahead)
+            if ahead == last:
+                round_w2(on_scalar, 1)
+            if opens_pair:
+                round_w1(on_vector, 1, 0, W1_ON_VECTOR[1])
+            scale(step)
+            if opens_pair:
+                quantize_w1(1)
+            if ahead >= CHUNKS:
+                quantize_x(ahead)
+                first_layer(ahead)
+            if step % 2 == 1:
+                if step == 1:
+                    quantize_w2(0)
+                quantize_h(step - 1, 0, 2 * SIDE)
+                if ahead == last:
+                    quantize_w2(1)
+                second_layer(step - 1)
+                second_layer(step)
+            else:
+                add_residual(step - 2, 2)
+                if step == CHUNKS:
+                    store(0, CHUNKS)
+
+        for step in (last - 1, last):
+            gelu(step, 0)
+            gelu(step, 1)
+        scale(last - 1, 0, 1)
+        scale(last - 1, 1, 2)
+        add_residual(last - 3, 2)
+        store(last - 3, 2)
+        quantize_h(last - 1, 0, SIDE)
+        second_layer(last - 1)
+        scale(last, 0, 1)
+        scale(last, 1, 2)
+        for c in range(SIDE):
+            quantize_h(last, c, c + 1)
+            second_layer(last, c, c + 1)
+        for step in (last - 1, last):
+            add_residual(step, 1)
+            store(step, 1)

from contextlib import ExitStack

import concourse.mybir as mybir

G, D, K, M, N = 4, 256, 512, 128, 512
FLOPS = 2 * G * N * (D * K + K * M)

F32 = mybir.dt.float32
BF16 = mybir.dt.bfloat16
U32 = mybir.dt.uint32
U8 = mybir.dt.uint8
FP8X4 = mybir.dt.float8_e4m3fn_x4
ALU = mybir.AluOpType
ACT = mybir.ActivationFunctionType

P = 128
PACK = 4
ROWS = D // PACK
SIDE = P // ROWS
CH = 128
CHUNKS = N // CH
STEPS = G // SIDE * CHUNKS
UNIT = PACK * CH
Z_BANKS = 3
AHEAD = 2
HS_ROW = 8
W1_ON_VECTOR = (76, 36)


def tile_rows_gmlp_gelu_res_kernel(tc, x, w1, hs, w2, r, out):
    nc = tc.nc
    with ExitStack() as ctx:
        sb = ctx.enter_context(tc.tile_pool(name="sb", bufs=1))
        ps = ctx.enter_context(tc.psum_pool(name="ps", bufs=1))
        ctx.enter_context(tc.manual_schedule())

        def sbuf(name, shape, dtype):
            return sb.tile(shape, dtype, name=name, align_bytes=64)

        def quantize(name, values, words):
            codes = sbuf(name + "_codes", [P, words], U32)
            scales = sbuf(name + "_scales", [P, words], U8)
            nc.vector.quantize_mx(out=codes[:].bitcast(FP8X4), scales=scales[:], in_=values)
            return codes, scales

        def multiply(sums, weights, moving, partitions, columns):
            nc.tensor.matmul_mx(
                out=sums,
                lhsT=weights[0][partitions, columns].bitcast(FP8X4),
                lhsT_scale=weights[1][partitions, columns],
                rhs=moving[0][partitions, :].bitcast(FP8X4),
                rhs_scale=moving[1][partitions, :],
                start=True,
                stop=True,
            )

        on_vector, on_scalar = nc.vector.tensor_copy, nc.scalar.copy

        z_banks = [[ps.tile([P, UNIT], F32, name="z%d_%d" % (c, b)) for b in range(Z_BANKS)] for c in range(SIDE)]
        y_banks = [ps.tile([P, SIDE * 2 * CH], F32, name="y%d" % b) for b in range(2)]

        w1_raw, w1_bf, w1_mx = {}, {}, {}
        x_raw, x_bf, x_mx = {}, {}, {}
        w2_raw, w2_bf, w2_mx = {}, {}, {}
        hs_sb, r_sb, result = {}, {}, {}
        act, h_bf, h_mx = {}, {}, {}

        def groups(pair):
            return slice(SIDE * pair, SIDE * (pair + 1))

        def y_bank(step):
            turn = step // 2 + (step == STEPS - 1)
            return y_banks[turn % 2][:].rearrange("p (c n) -> p c n", c=SIDE)

        def load_w1(pair):
            w1_raw[pair] = sbuf("w1_raw%d" % pair, [P, PACK, K], F32)
            w1_bf[pair] = sbuf("w1_bf%d" % pair, [P, PACK * K], BF16)
            nc.sync.dma_start(out=w1_raw[pair][:], in_=w1[groups(pair)].rearrange("c (p j) k -> (c p) j k", j=PACK))

        def load_x(step, count):
            pair, chunk = divmod(step, CHUNKS)
            raw = sbuf("x_raw%d" % step, [P, PACK, count * CH], F32)
            rows = x[groups(pair)].rearrange("c (p j) n -> (c p) j n", j=PACK)
            nc.sync.dma_start(out=raw[:], in_=rows[:, :, chunk * CH:(chunk + count) * CH])
            for i in range(count):
                x_raw[step + i] = (raw, i * CH)

        def load_hs(pair):
            hs_sb[pair] = sbuf("hs%d" % pair, [P, SIDE, HS_ROW], F32)
            nc.sync.dma_start(out=hs_sb[pair][:, :, 0:PACK], in_=hs[groups(pair)].rearrange("c (s t) o -> s c (t o)", t=PACK))

        def load_w2(pair):
            w2_raw[pair] = sbuf("w2_raw%d" % pair, [P, SIDE, PACK * M], F32)
            nc.sync.dma_start(out=w2_raw[pair][:], in_=w2[groups(pair)].rearrange("c (s t) m -> s c (t m)", t=PACK))

        def load_r(pair):
            r_sb[pair] = sbuf("r%d" % pair, [P, SIDE, N], F32)
            result[pair] = sbuf("result%d" % pair, [P, SIDE, N], F32)
            nc.sync.dma_start(out=r_sb[pair][:], in_=r[groups(pair)].rearrange("c m n -> m c n"))

        def store(step, count):
            pair, chunk = divmod(step, CHUNKS)
            cols = slice(chunk * CH, (chunk + count) * CH)
            nc.sync.dma_start(out=out[groups(pair)].rearrange("c m n -> m c n")[:, :, cols], in_=result[pair][:, :, cols])

        def round_w1(copy, pair, lo, hi):
            dealt = w1_bf[pair][:].rearrange("p (t s j) -> p s j t", t=PACK, j=PACK)
            raw = w1_raw[pair][:].rearrange("p j (s t) -> p s j t", t=PACK)
            copy(out=dealt[:, lo:hi], in_=raw[:, lo:hi])

        def round_x(copy, step, count=1):
            if step % 2 == 0:
                x_bf[step // 2] = sbuf("x_bf%d" % step, [P, 2 * UNIT], BF16)
            at = step % 2 * UNIT
            raw, first = x_raw[step]
            copy(out=x_bf[step // 2][:, at:at + count * UNIT].rearrange("p (a e j) -> p a j e", e=2, j=PACK),
                 in_=raw[:, :, first:first + count * CH].rearrange("p j (a e) -> p a j e", e=2))

        def round_w2(copy, pair):
            w2_bf[pair] = sbuf("w2_bf%d" % pair, [P, SIDE * PACK * M], BF16)
            copy(out=w2_bf[pair][:].rearrange("p (c a e t) -> p c a t e", c=SIDE, e=2, t=PACK),
                 in_=w2_raw[pair][:].rearrange("p c (t a e) -> p c a t e", t=PACK, e=2))

        def quantize_w1(pair):
            w1_mx[pair] = quantize("w1_%d" % pair, w1_bf[pair][:], K)

        def quantize_w2(pair):
            w2_mx[pair] = quantize("w2_%d" % pair, w2_bf[pair][:], SIDE * M)

        def quantize_x(step, count=1):
            at = step % 2 * UNIT
            codes, scales = quantize("x_%d" % step, x_bf[step // 2][:, at:at + count * UNIT], count * CH)
            for i in range(count):
                x_mx[step + i] = (codes[:, i * CH:(i + 1) * CH], scales[:, i * CH:(i + 1) * CH])

        def first_layer(step):
            for t in range(PACK):
                for c in range(SIDE):
                    multiply(z_banks[c][step % Z_BANKS][:, t * CH:(t + 1) * CH], w1_mx[step // CHUNKS], x_mx[step],
                             slice(ROWS * c, ROWS * (c + 1)), slice(t * P, (t + 1) * P))

        def gelu(step, c):
            if step not in act:
                act[step] = sbuf("act%d" % step, [P, SIDE * UNIT], F32)
                if step % 2 == 0:
                    h_bf[step // 2] = sbuf("h_bf%d" % step, [P, 2 * SIDE * UNIT], BF16)
            nc.scalar.activation(out=act[step][:, c * UNIT:(c + 1) * UNIT].rearrange("p (n t) -> p n t", t=PACK),
                                 in_=z_banks[c][step % Z_BANKS][:].rearrange("p (t n) -> p n t", t=PACK),
                                 func=ACT.Gelu_apprx_tanh)

        def h_values(step, lo, hi):
            at = step % 2 * SIDE
            return h_bf[step // 2][:, (at + lo) * UNIT:(at + hi) * UNIT]

        def scale(step, lo=0, hi=SIDE):
            factors = hs_sb[step // CHUNKS][:, lo:hi, 0:PACK].unsqueeze(2).to_broadcast([P, hi - lo, CH, PACK])
            nc.vector.tensor_tensor(out=h_values(step, lo, hi).rearrange("p (c n t) -> p c n t", n=CH, t=PACK),
                                    in0=act[step][:, lo * UNIT:hi * UNIT].rearrange("p (c n t) -> p c n t", n=CH, t=PACK),
                                    in1=factors, op=ALU.mult)

        def quantize_h(step, lo, hi):
            codes, scales = quantize("h_%d_%d" % (step, lo), h_values(step, lo, hi), (hi - lo) * CH)
            for u in range(lo, hi):
                cols = slice((u - lo) * CH, (u - lo + 1) * CH)
                h_mx[step + u // SIDE, u % SIDE] = (codes[:, cols], scales[:, cols])

        def second_layer(step, lo=0, hi=SIDE):
            at = step % 2 * CH
            for c in range(lo, hi):
                multiply(y_bank(step)[:, c, at:at + CH], w2_mx[step // CHUNKS], h_mx[step, c],
                         slice(0, P), slice(c * M, (c + 1) * M))

        def add_residual(step, count):
            pair, chunk = divmod(step, CHUNKS)
            cols = slice(chunk * CH, (chunk + count) * CH)
            at = step % 2 * CH
            nc.vector.tensor_tensor(out=result[pair][:, :, cols], in0=y_bank(step)[:, :, at:at + count * CH],
                                    in1=r_sb[pair][:, :, cols], op=ALU.add)

        load_w1(0)
        load_x(0, 1)
        load_x(1, 1)
        load_x(2, 2)
        load_hs(0)
        load_w2(0)
        load_w1(1)
        load_x(4, 2)
        load_r(0)
        load_hs(1)
        load_x(6, 2)
        load_w2(1)
        load_r(1)

        round_w1(on_vector, 0, 0, W1_ON_VECTOR[0])
        round_w1(on_scalar, 0, W1_ON_VECTOR[0], P)
        round_x(on_vector, 0)
        quantize_w1(0)
        quantize_x(0)
        first_layer(0)
        round_x(on_vector, 1)
        quantize_x(1)
        first_layer(1)
        round_x(on_vector, 2, 2)

        gelu(0, 0)
        gelu(0, 1)
        scale(0, 0, 1)
        quantize_x(2, 2)
        first_layer(2)
        first_layer(3)
        scale(0, 1, 2)
        round_w2(on_vector, 0)

        last = STEPS - 1
        for step in range(1, last - 1):
            ahead = step + AHEAD
            opens_pair = ahead == CHUNKS
            gelu(step, 0)
            gelu(step, 1)
            if opens_pair:
                round_w1(on_scalar, 1, W1_ON_VECTOR[1], P)
            if ahead >= CHUNKS:
                round_x(on_scalar, ahead)
            if ahead == last:
                round_w2(on_scalar, 1)
            if opens_pair:
                round_w1(on_vector, 1, 0, W1_ON_VECTOR[1])
            scale(step)
            if opens_pair:
                quantize_w1(1)
            if ahead >= CHUNKS:
                quantize_x(ahead)
                first_layer(ahead)
            if step % 2 == 1:
                if step == 1:
                    quantize_w2(0)
                quantize_h(step - 1, 0, 2 * SIDE)
                if ahead == last:
                    quantize_w2(1)
                second_layer(step - 1)
                second_layer(step)
            else:
                add_residual(step - 2, 2)
                if step == CHUNKS:
                    store(0, CHUNKS)

        for step in (last - 1, last):
            gelu(step, 0)
            gelu(step, 1)
        scale(last - 1, 0, 1)
        scale(last - 1, 1, 2)
        add_residual(last - 3, 2)
        store(last - 3, 2)
        quantize_h(last - 1, 0, SIDE)
        second_layer(last - 1)
        scale(last, 0, 1)
        scale(last, 1, 2)
        for c in range(SIDE):
            quantize_h(last, c, c + 1)
            second_layer(last, c, c + 1)
        for step in (last - 1, last):
            add_residual(step, 1)
            store(step, 1)
